import numpy as np
import ml_dtypes


def mxq(x, axis, fmt="e4m3"):
    dtype, down = {"e4m3": (ml_dtypes.float8_e4m3fn, 7), "e5m2": (ml_dtypes.float8_e5m2, 14)}[fmt]
    v = np.moveaxis(np.asarray(x, np.float32).astype(ml_dtypes.bfloat16).astype(np.float64), axis, -1)
    blocks = v.reshape(v.shape[:-1] + (-1, 32))
    amax = np.abs(blocks).max(-1, keepdims=True)
    byte = np.maximum(np.where(amax > 0, np.frexp(amax)[1] - 1 + 127, 0) - down, 1)
    scale = np.exp2(byte - 127.0)
    codes = (blocks / scale).astype(np.float32).astype(dtype).astype(np.float64)
    return np.moveaxis((codes * scale).reshape(v.shape), -1, axis)


WIDE = False


def mx_kscale(k):
    if not WIDE:
        return np.ones(k)
    levels = np.array([10, -10, 5, -5, 0])
    if k % 512:
        return np.exp2(np.random.permutation(np.resize(levels, k // 32))).repeat(32)
    a = np.empty((k // 512, 16))
    for p in range(k // 512):
        a[p, :8] = np.random.permutation(np.resize(levels, 8))
        for g in range(8):
            far = levels[np.abs(levels - a[p, g]) >= 10]
            a[p, g + 8] = far[np.random.randint(len(far))]
    return np.exp2(a.ravel()).repeat(32)


def f64(x):
    return np.asarray(x).astype(np.float64)


def striped(idx):
    return np.tile(idx.reshape(-1, 16).T, (8, 1)).astype(np.uint16)


def unstriped(offs):
    return offs[:16].T.reshape(-1).astype(np.int64)


def pack_weight(w):
    k, n = w.shape
    w = f64(np.asarray(w, np.float32).astype(ml_dtypes.bfloat16)).reshape(k // 32, 32, n)
    amax = np.abs(w).max(1)
    byte = np.clip(np.where(amax > 0, np.frexp(amax)[1] - 1 + 127 - 7, 1), 1, 254)
    scaled = (w * np.exp2(127.0 - byte)[:, None, :]).reshape(k, n).astype(np.float32)
    words = np.ascontiguousarray(scaled.reshape(k // 512, 128, 4, n).transpose(0, 1, 3, 2)).astype(ml_dtypes.float8_e4m3fn).view(np.uint8)
    return words, np.ascontiguousarray(byte.astype(np.uint8).reshape(k // 512, 16, n))


def unpack_weight(words, scales):
    g, p, n, _ = words.shape
    vals = np.ascontiguousarray(words).view(ml_dtypes.float8_e4m3fn).astype(np.float64) * np.repeat(np.exp2(scales.astype(np.float64) - 127.0), 8, axis=1)[..., None]
    return vals.transpose(0, 1, 3, 2).reshape(g * 512, n)


K, T, S, N, V = 512, 1024, 512, 128, 256


def setup_inputs():
    n = np.random.standard_normal
    s = mx_kscale(K)[:, None]
    packed_xT = pack_weight(n((K, T)) * s)
    return {
        "x_words": packed_xT[0],
        "x_scales": packed_xT[1],
        "w1": (n((K, N)) / np.sqrt(K) / s).astype(np.float32),
        "w2": (n((K, N)) / np.sqrt(K) / s).astype(np.float32),
        "noise": (np.random.uniform(0.2, 0.8, (N, 1))).astype(np.float32),
        "rxa": (n((N, V))).astype(np.float32),
        "rxb": (n((N, V))).astype(np.float32),
        "offs": striped(np.random.permutation(T)[:S]),
        "st1": striped(np.random.randint(0, S, V)),
        "st2": striped(np.random.randint(0, S, V)),
    }


def reference(x_words, x_scales, w1, w2, noise, rxa, rxb, offs, st1, st2):
    xq = unpack_weight(x_words, x_scales)[:, unstriped(offs)]
    ha = mxq(f64(w1), 0, "e4m3").T @ xq
    hab = ha[:, unstriped(st2)]
    hb = mxq(f64(w2), 0, "e4m3").T @ xq
    hbb = hb[:, unstriped(st2)]
    gb = (hab) ** 2 + (hbb) ** 2 + f64(noise)
    haa = ha[:, unstriped(st1)]
    hba = hb[:, unstriped(st1)]
    ma = haa * f64(rxa) + hba * f64(rxb)
    gx = haa * hab + hba * hbb
    mb = hab * f64(rxa) + hbb * f64(rxb)
    ga = (haa) ** 2 + (hba) ** 2 + f64(noise)
    det = ga * gb - ((gx) ** 2)
    return (gb * ma - (gx * mb)) / det

@@ -1,0 +1,143 @@
+from contextlib import ExitStack
+
+import concourse.mybir as mybir
+from concourse.masks import make_identity
+
+K, T, S, N, V = 512, 1024, 512, 128, 256
+FLOPS = 2 * 2 * K * N * S
+
+F32 = mybir.dt.float32
+BF16 = mybir.dt.bfloat16
+I32 = mybir.dt.int32
+U32 = mybir.dt.uint32
+U16 = mybir.dt.uint16
+U8 = mybir.dt.uint8
+FP8X4 = mybir.dt.float8_e4m3fn_x4
+ALU = mybir.AluOpType
+ACT = mybir.ActivationFunctionType
+
+P = 128
+
+
+def tile_picked_ylmm2_est_p_kernel(tc, x_words, x_scales, w1, w2, noise, rxa, rxb, offs, st1, st2, out):
+    nc = tc.nc
+    with ExitStack() as ctx:
+        keep = ctx.enter_context(tc.tile_pool(name="keep", bufs=1))
+        psum = ctx.enter_context(tc.psum_pool(name="psum", bufs=1))
+
+        offs_sb = keep.tile([P, S // 16], U16, name="offs_sb")
+        st1_sb = keep.tile([P, V // 16], U16, name="st1_sb")
+        st2_sb = keep.tile([P, V // 16], U16, name="st2_sb")
+        words_all = keep.tile([P, T], U32, name="words_all", align_bytes=64)
+        scales_all = keep.tile([P, T], U8, name="scales_all", tag="plane", align_bytes=64)
+        w_raw = [keep.tile([P, 4, N], F32, name=f"w_raw{i}", align_bytes=64) for i in range(2)]
+        noise_sb = keep.tile([P, 1], F32, name="noise_sb")
+        rx = keep.tile([P, 2, V], F32, name="rx")
+        warm = keep.tile([P, 2], F32, name="warm")
+
+        ident = keep.tile([P, P], F32, name="ident", align_bytes=64)
+        half = keep.tile([P, 1], F32, name="half")
+        nc.vector.memset(scales_all[:].bitcast(I32), 0)
+        nc.sync.dma_start(offs_sb[:], offs)
+        nc.sync.dma_start(w_raw[0][:], w1.rearrange("(p j) n -> p j n", j=4))
+        for q, queue in enumerate((nc.sync, nc.sync, nc.scalar, nc.scalar)):
+            queue.dma_start(scales_all[32 * q : 32 * q + 4, :].bitcast(I32), x_scales[0, 4 * q : 4 * q + 4, :].bitcast(I32))
+        nc.sync.dma_start(words_all[:].bitcast(I32), x_words[0].rearrange("p c r -> p (c r)").bitcast(I32))
+        nc.sync.dma_start(w_raw[1][:], w2.rearrange("(p j) n -> p j n", j=4))
+        nc.sync.dma_start(noise_sb[:], noise)
+        nc.sync.dma_start(rx[:, 0, :], rxa)
+        nc.sync.dma_start(st1_sb[:], st1)
+        nc.sync.dma_start(rx[:, 1, :], rxb)
+        nc.sync.dma_start(st2_sb[:], st2)
+        nc.vector.memset(warm[:, 0:1], 1.0)
+        nc.scalar.activation(warm[:, 1:2], warm[:, 0:1], ACT.Abs_reciprocal_sqrt)
+        make_identity(nc, ident[:])
+        nc.gpsimd.memset(half[:], 0.5)
+        root = keep.tile([P, 1], F32, name="root")
+        nc.gpsimd.tensor_tensor(root[:], noise_sb[:], half[:], ALU.pow)
+        noise2 = keep.tile([P, 1], F32, name="noise2")
+        nc.gpsimd.tensor_tensor(noise2[:], noise_sb[:], noise_sb[:], ALU.mult)
+
+        x_sc = keep.tile([P, S], U8, name="x_sc", align_bytes=64)
+        nc.vector.tensor_copy(x_sc[:], scales_all[:].indirect(offs_sb[:]))
+
+        w_bf = [keep.tile([P, N, 4], BF16, name=f"w_bf{i}", align_bytes=64) for i in range(2)]
+        w_q = [keep.tile([P, N], U32, name=f"w_q{i}", align_bytes=64) for i in range(2)]
+        w_sc = [keep.tile([P, N], U8, name=f"w_sc{i}", tag=("plane", "w_sc1")[i], align_bytes=64) for i in range(2)]
+        x_q = keep.tile([P, S], U32, name="x_q", align_bytes=64)
+        h_sb = [keep.tile([P, S], F32, name=f"h_sb{i}", align_bytes=64) for i in range(2)]
+        for i in range(2):
+            nc.scalar.copy(w_bf[i][:], w_raw[i][:].rearrange("p j n -> p n j"))
+
+        def quantize(i):
+            nc.vector.quantize_mx(out=w_q[i][:].bitcast(FP8X4), scales=w_sc[i][:], in_=w_bf[i][:].rearrange("p n j -> p (n j)"))
+
+        def pick(cols):
+            nc.vector.tensor_copy(x_q[:, cols], words_all[:].indirect(offs_sb[:, cols.start // 16 : cols.stop // 16]))
+
+        def product(i, cols):
+            acc = psum.tile([P, cols.stop - cols.start], F32, name=f"acc{i}_{cols.start}")
+            nc.tensor.matmul_mx(out=acc[:], lhsT=w_q[i][:].bitcast(FP8X4), lhsT_scale=w_sc[i][:], rhs=x_q[:, cols].bitcast(FP8X4), rhs_scale=x_sc[:, cols], start=True, stop=True)
+            nc.scalar.copy(h_sb[i][:, cols], acc[:])
+
+        pieces = (slice(0, 256), slice(256, 384), slice(384, 512))
+        quantize(0)
+        for cols in pieces:
+            pick(cols)
+            product(0, cols)
+        quantize(1)
+        product(1, slice(0, S))
+
+        nrx = keep.tile([P, 2, V], F32, name="nrx")
+        nc.vector.tensor_scalar(nrx[:], rx[:], noise_sb[:, 0:1], None, ALU.mult)
+
+        g = keep.tile([P, 4, V], F32, name="g")
+        sq = keep.tile([P, 4, V], F32, name="sq", align_bytes=64)
+        det_t = [psum.tile([P, P], F32, name=f"det_t{b}") for b in range(2)]
+        blocks = [slice(b * P, (b + 1) * P) for b in range(2)]
+        order = ((0, 0, st1_sb), (3, 0, st2_sb), (2, 1, st2_sb), (1, 1, st1_sb))
+        for n, (slot, i, lst) in enumerate(order):
+            nc.vector.tensor_copy(g[:, slot, :], h_sb[i][:].indirect(lst[:]))
+            nc.scalar.activation(sq[:, slot, :], g[:, slot, :], ACT.Square, scale=root[:, 0:1])
+            for b in range(2):
+                nc.tensor.matmul(det_t[b][:], sq[:, slot, blocks[b]], ident[:], is_transpose=True, start=(n == 0), stop=False)
+                if n == 0:
+                    nc.tensor.matmul(det_t[b][:], noise2[:, 0:1].to_broadcast([P, P]), ident[:], is_transpose=True, start=False, stop=False)
+
+        pc = [keep.tile([P, 2, P], F32, name=f"pc{b}", tag=("held", "pc1")[b]) for b in range(2)]
+        c = keep.tile([P, V], F32, name="c")
+        d = keep.tile([P, V], F32, name="d")
+        ma = keep.tile([P, V], F32, name="ma")
+        csq = keep.tile([P, V], F32, name="csq", align_bytes=64)
+        rs_t = keep.tile([P, 2, P], F32, name="rs_t")
+        inv_t = keep.tile([P, 2, P], F32, name="inv_t", align_bytes=64)
+        inv = [psum.tile([P, P], F32, name=f"inv{b}") for b in range(2)]
+        prod = keep.tile([P, V], F32, name="prod")
+        num = keep.tile([P, V], F32, name="num")
+        res = keep.tile([P, V], F32, name="res")
+        for t in range(2):
+            for b in range(2):
+                nc.vector.tensor_tensor(pc[b][:, t, :], g[:, t, blocks[b]], g[:, 2 + t, blocks[b]], ALU.mult)
+        for b in range(2):
+            nc.vector.tensor_tensor(c[:, blocks[b]], pc[b][:, 0, :], pc[b][:, 1, :], ALU.subtract)
+            nc.scalar.activation(csq[:, blocks[b]], c[:, blocks[b]], ACT.Square)
+            nc.tensor.matmul(det_t[b][:], csq[:, blocks[b]], ident[:], is_transpose=True, start=False, stop=True)
+        for b in range(2):
+            nc.scalar.activation(rs_t[:, b, :], det_t[b][:], ACT.Abs_reciprocal_sqrt)
+        for b in range(2):
+            nc.scalar.activation(inv_t[:, b, :], rs_t[:, b, :], ACT.Square)
+            nc.tensor.transpose(inv[b][:], inv_t[:, b, :], ident[:])
+        late = keep.tile([P, 4, V], F32, name="late", tag="held")
+        pd = late[:, 0:2, :]
+        pm = late[:, 2:4, :]
+        nc.vector.tensor_tensor(pd, rx[:], g[:, 2:4, :], ALU.mult)
+        nc.vector.tensor_tensor(pm, nrx[:], g[:, 0:2, :], ALU.mult)
+        nc.vector.tensor_tensor(d[:], pd[:, 0, :], pd[:, 1, :], ALU.subtract)
+        nc.vector.tensor_tensor(ma[:], pm[:, 0, :], pm[:, 1, :], ALU.add)
+        for b in range(2):
+            nc.vector.tensor_tensor(prod[:, blocks[b]], c[:, blocks[b]], d[:, blocks[b]], ALU.mult)
+        for b in range(2):
+            nc.vector.tensor_tensor(num[:, blocks[b]], prod[:, blocks[b]], ma[:, blocks[b]], ALU.add)
+        for b, queue in enumerate((nc.sync, nc.scalar)):
+            nc.vector.tensor_tensor(res[:, blocks[b]], num[:, blocks[b]], inv[b][:], ALU.mult)
+            queue.dma_start(out[:, blocks[b]], res[:, blocks[b]])

@@ -29,45 +29,47 @@ def tile_picked_ylmm2_est_p_kernel(tc, x_words, x_scales, w1, w2, noise, rxa, rx
         st1_sb = keep.tile([P, V // 16], U16, name="st1_sb")
         st2_sb = keep.tile([P, V // 16], U16, name="st2_sb")
         words_all = keep.tile([P, T], U32, name="words_all", align_bytes=64)
-        scales_all = keep.tile([P, T], U8, name="scales_all", tag="plane", align_bytes=64)
+        scales_all = keep.tile([P, T], U8, name="scales_all", align_bytes=64)
         w_raw = [keep.tile([P, 4, N], F32, name=f"w_raw{i}", align_bytes=64) for i in range(2)]
         noise_sb = keep.tile([P, 1], F32, name="noise_sb")
         rx = keep.tile([P, 2, V], F32, name="rx")
         warm = keep.tile([P, 2], F32, name="warm")
 
         ident = keep.tile([P, P], F32, name="ident", align_bytes=64)
-        half = keep.tile([P, 1], F32, name="half")
         nc.vector.memset(scales_all[:].bitcast(I32), 0)
         nc.sync.dma_start(offs_sb[:], offs)
-        nc.sync.dma_start(w_raw[0][:], w1.rearrange("(p j) n -> p j n", j=4))
         for q, queue in enumerate((nc.sync, nc.sync, nc.scalar, nc.scalar)):
             queue.dma_start(scales_all[32 * q : 32 * q + 4, :].bitcast(I32), x_scales[0, 4 * q : 4 * q + 4, :].bitcast(I32))
+        nc.sync.dma_start(w_raw[0][:], w1.rearrange("(p j) n -> p j n", j=4))
         nc.sync.dma_start(words_all[:].bitcast(I32), x_words[0].rearrange("p c r -> p (c r)").bitcast(I32))
         nc.sync.dma_start(w_raw[1][:], w2.rearrange("(p j) n -> p j n", j=4))
         nc.sync.dma_start(noise_sb[:], noise)
-        nc.sync.dma_start(rx[:, 0, :], rxa)
         nc.sync.dma_start(st1_sb[:], st1)
-        nc.sync.dma_start(rx[:, 1, :], rxb)
         nc.sync.dma_start(st2_sb[:], st2)
+        nc.sync.dma_start(rx[:, 0, :], rxa)
+        nc.sync.dma_start(rx[:, 1, :], rxb)
         nc.vector.memset(warm[:, 0:1], 1.0)
         nc.scalar.activation(warm[:, 1:2], warm[:, 0:1], ACT.Abs_reciprocal_sqrt)
-        make_identity(nc, ident[:])
-        nc.gpsimd.memset(half[:], 0.5)
-        root = keep.tile([P, 1], F32, name="root")
-        nc.gpsimd.tensor_tensor(root[:], noise_sb[:], half[:], ALU.pow)
-        noise2 = keep.tile([P, 1], F32, name="noise2")
-        nc.gpsimd.tensor_tensor(noise2[:], noise_sb[:], noise_sb[:], ALU.mult)
+        nc.vector.memset(ident[:], 0.0)
+        make_identity(nc, ident[:], nomemset=True)
 
         x_sc = keep.tile([P, S], U8, name="x_sc", align_bytes=64)
         nc.vector.tensor_copy(x_sc[:], scales_all[:].indirect(offs_sb[:]))
 
         w_bf = [keep.tile([P, N, 4], BF16, name=f"w_bf{i}", align_bytes=64) for i in range(2)]
         w_q = [keep.tile([P, N], U32, name=f"w_q{i}", align_bytes=64) for i in range(2)]
-        w_sc = [keep.tile([P, N], U8, name=f"w_sc{i}", tag=("plane", "w_sc1")[i], align_bytes=64) for i in range(2)]
+        w_sc = [keep.tile([P, N], U8, name=f"w_sc{i}", align_bytes=64) for i in range(2)]
         x_q = keep.tile([P, S], U32, name="x_q", align_bytes=64)
         h_sb = [keep.tile([P, S], F32, name=f"h_sb{i}", align_bytes=64) for i in range(2)]
         for i in range(2):
             nc.scalar.copy(w_bf[i][:], w_raw[i][:].rearrange("p j n -> p n j"))
+
+        inv_root = keep.tile([P, 1], F32, name="inv_root")
+        root = keep.tile([P, 1], F32, name="root")
+        noise2 = keep.tile([P, 1], F32, name="noise2")
+        nc.scalar.activation(inv_root[:], noise_sb[:], ACT.Abs_reciprocal_sqrt, bias=1e-30)
+        nc.scalar.activation(noise2[:], noise_sb[:], ACT.Square)
+        nc.scalar.activation(root[:], inv_root[:], ACT.Copy, scale=noise_sb[:, 0:1])
 
         def quantize(i):
             nc.vector.quantize_mx(out=w_q[i][:].bitcast(FP8X4), scales=w_sc[i][:], in_=w_bf[i][:].rearrange("p n j -> p (n j)"))

@@ -33,25 +33,29 @@ def tile_picked_ylmm2_est_p_kernel(tc, x_words, x_scales, w1, w2, noise, rxa, rx
         w_raw = [keep.tile([P, 4, N], F32, name=f"w_raw{i}", align_bytes=64) for i in range(2)]
         noise_sb = keep.tile([P, 1], F32, name="noise_sb")
         rx = keep.tile([P, 2, V], F32, name="rx")
-        warm = keep.tile([P, 2], F32, name="warm")
 
         ident = keep.tile([P, P], F32, name="ident", align_bytes=64)
         nc.vector.memset(scales_all[:].bitcast(I32), 0)
         nc.sync.dma_start(offs_sb[:], offs)
+        nc.sync.dma_start(noise_sb[:], noise)
         for q, queue in enumerate((nc.sync, nc.sync, nc.scalar, nc.scalar)):
             queue.dma_start(scales_all[32 * q : 32 * q + 4, :].bitcast(I32), x_scales[0, 4 * q : 4 * q + 4, :].bitcast(I32))
         nc.sync.dma_start(w_raw[0][:], w1.rearrange("(p j) n -> p j n", j=4))
         nc.sync.dma_start(words_all[:].bitcast(I32), x_words[0].rearrange("p c r -> p (c r)").bitcast(I32))
         nc.sync.dma_start(w_raw[1][:], w2.rearrange("(p j) n -> p j n", j=4))
-        nc.sync.dma_start(noise_sb[:], noise)
         nc.sync.dma_start(st1_sb[:], st1)
         nc.sync.dma_start(st2_sb[:], st2)
         nc.sync.dma_start(rx[:, 0, :], rxa)
         nc.sync.dma_start(rx[:, 1, :], rxb)
-        nc.vector.memset(warm[:, 0:1], 1.0)
-        nc.scalar.activation(warm[:, 1:2], warm[:, 0:1], ACT.Abs_reciprocal_sqrt)
         nc.vector.memset(ident[:], 0.0)
         make_identity(nc, ident[:], nomemset=True)
+
+        inv_root = keep.tile([P, 1], F32, name="inv_root")
+        root = keep.tile([P, 1], F32, name="root")
+        noise2 = keep.tile([P, 1], F32, name="noise2")
+        nc.scalar.activation(inv_root[:], noise_sb[:], ACT.Abs_reciprocal_sqrt, bias=1e-30)
+        nc.scalar.activation(noise2[:], noise_sb[:], ACT.Square)
+        nc.scalar.activation(root[:], inv_root[:], ACT.Copy, scale=noise_sb[:, 0:1])
 
         x_sc = keep.tile([P, S], U8, name="x_sc", align_bytes=64)
         nc.vector.tensor_copy(x_sc[:], scales_all[:].indirect(offs_sb[:]))
@@ -63,13 +67,6 @@ def tile_picked_ylmm2_est_p_kernel(tc, x_words, x_scales, w1, w2, noise, rxa, rx
         h_sb = [keep.tile([P, S], F32, name=f"h_sb{i}", align_bytes=64) for i in range(2)]
         for i in range(2):
             nc.scalar.copy(w_bf[i][:], w_raw[i][:].rearrange("p j n -> p n j"))
-
-        inv_root = keep.tile([P, 1], F32, name="inv_root")
-        root = keep.tile([P, 1], F32, name="root")
-        noise2 = keep.tile([P, 1], F32, name="noise2")
-        nc.scalar.activation(inv_root[:], noise_sb[:], ACT.Abs_reciprocal_sqrt, bias=1e-30)
-        nc.scalar.activation(noise2[:], noise_sb[:], ACT.Square)
-        nc.scalar.activation(root[:], inv_root[:], ACT.Copy, scale=noise_sb[:, 0:1])
 
         def quantize(i):
             nc.vector.quantize_mx(out=w_q[i][:].bitcast(FP8X4), scales=w_sc[i][:], in_=w_bf[i][:].rearrange("p n j -> p (n j)"))
@@ -88,10 +85,9 @@ def tile_picked_ylmm2_est_p_kernel(tc, x_words, x_scales, w1, w2, noise, rxa, rx
             pick(cols)
             product(0, cols)
         quantize(1)
-        product(1, slice(0, S))
+        product(1, slice(0, 256))
+        product(1, slice(256, 512))
 
-        nrx = keep.tile([P, 2, V], F32, name="nrx")
-        nc.vector.tensor_scalar(nrx[:], rx[:], noise_sb[:, 0:1], None, ALU.mult)
 
         g = keep.tile([P, 4, V], F32, name="g")
         sq = keep.tile([P, 4, V], F32, name="sq", align_bytes=64)
@@ -113,7 +109,7 @@ def tile_picked_ylmm2_est_p_kernel(tc, x_words, x_scales, w1, w2, noise, rxa, rx
         csq = keep.tile([P, V], F32, name="csq", align_bytes=64)
         rs_t = keep.tile([P, 2, P], F32, name="rs_t")
         inv_t = keep.tile([P, 2, P], F32, name="inv_t", align_bytes=64)
-        inv = [psum.tile([P, P], F32, name=f"inv{b}") for b in range(2)]
+        inv = [psum.tile([P, P], F32, name=f"inv{b}", tag=("acc0_0", "acc0_256")[b]) for b in range(2)]
         prod = keep.tile([P, V], F32, name="prod")
         num = keep.tile([P, V], F32, name="num")
         res = keep.tile([P, V], F32, name="res")
@@ -133,13 +129,13 @@ def tile_picked_ylmm2_est_p_kernel(tc, x_words, x_scales, w1, w2, noise, rxa, rx
         pd = late[:, 0:2, :]
         pm = late[:, 2:4, :]
         nc.vector.tensor_tensor(pd, rx[:], g[:, 2:4, :], ALU.mult)
-        nc.vector.tensor_tensor(pm, nrx[:], g[:, 0:2, :], ALU.mult)
+        nc.vector.tensor_tensor(pm, rx[:], g[:, 0:2, :], ALU.mult)
         nc.vector.tensor_tensor(d[:], pd[:, 0, :], pd[:, 1, :], ALU.subtract)
         nc.vector.tensor_tensor(ma[:], pm[:, 0, :], pm[:, 1, :], ALU.add)
         for b in range(2):
             nc.vector.tensor_tensor(prod[:, blocks[b]], c[:, blocks[b]], d[:, blocks[b]], ALU.mult)
         for b in range(2):
-            nc.vector.tensor_tensor(num[:, blocks[b]], prod[:, blocks[b]], ma[:, blocks[b]], ALU.add)
+            nc.vector.scalar_tensor_tensor(num[:, blocks[b]], ma[:, blocks[b]], noise_sb[:, 0:1], prod[:, blocks[b]], ALU.mult, ALU.add)
         for b, queue in enumerate((nc.sync, nc.scalar)):
             nc.vector.tensor_tensor(res[:, blocks[b]], num[:, blocks[b]], inv[b][:], ALU.mult)
             queue.dma_start(out[:, blocks[b]], res[:, blocks[b]])

@@ -49,6 +49,8 @@ def tile_picked_ylmm2_est_p_kernel(tc, x_words, x_scales, w1, w2, noise, rxa, rx
         nc.sync.dma_start(rx[:, 1, :], rxb)
         nc.vector.memset(ident[:], 0.0)
         make_identity(nc, ident[:], nomemset=True)
+        minus = keep.tile([P, 1], F32, name="minus", tag="held")
+        nc.vector.memset(minus[:], -1.0)
 
         inv_root = keep.tile([P, 1], F32, name="inv_root")
         root = keep.tile([P, 1], F32, name="root")
@@ -91,51 +93,57 @@ def tile_picked_ylmm2_est_p_kernel(tc, x_words, x_scales, w1, w2, noise, rxa, rx
 
         g = keep.tile([P, 4, V], F32, name="g")
         sq = keep.tile([P, 4, V], F32, name="sq", align_bytes=64)
-        det_t = [psum.tile([P, P], F32, name=f"det_t{b}") for b in range(2)]
+        power_t = [psum.tile([P, P], F32, name=f"power_t{b}") for b in range(2)]
         blocks = [slice(b * P, (b + 1) * P) for b in range(2)]
         order = ((0, 0, st1_sb), (3, 0, st2_sb), (2, 1, st2_sb), (1, 1, st1_sb))
         for n, (slot, i, lst) in enumerate(order):
             nc.vector.tensor_copy(g[:, slot, :], h_sb[i][:].indirect(lst[:]))
             nc.scalar.activation(sq[:, slot, :], g[:, slot, :], ACT.Square, scale=root[:, 0:1])
             for b in range(2):
-                nc.tensor.matmul(det_t[b][:], sq[:, slot, blocks[b]], ident[:], is_transpose=True, start=(n == 0), stop=False)
-                if n == 0:
-                    nc.tensor.matmul(det_t[b][:], noise2[:, 0:1].to_broadcast([P, P]), ident[:], is_transpose=True, start=False, stop=False)
+                nc.tensor.matmul(power_t[b][:], sq[:, slot, blocks[b]], ident[:], is_transpose=True, start=(n == 0), stop=(n == 3))
 
-        pc = [keep.tile([P, 2, P], F32, name=f"pc{b}", tag=("held", "pc1")[b]) for b in range(2)]
+        early = keep.tile([P, 2, V], F32, name="early")
+        nc.gpsimd.tensor_tensor(early[:, 0, :], rx[:, 0, :], g[:, 0, :], ALU.mult)
+        nc.gpsimd.tensor_tensor(early[:, 1, :], rx[:, 1, :], g[:, 3, :], ALU.mult)
+        pc = keep.tile([P, 2, V], F32, name="pc", align_bytes=64)
         c = keep.tile([P, V], F32, name="c")
         d = keep.tile([P, V], F32, name="d")
         ma = keep.tile([P, V], F32, name="ma")
-        csq = keep.tile([P, V], F32, name="csq", align_bytes=64)
-        rs_t = keep.tile([P, 2, P], F32, name="rs_t")
-        inv_t = keep.tile([P, 2, P], F32, name="inv_t", align_bytes=64)
-        inv = [psum.tile([P, P], F32, name=f"inv{b}", tag=("acc0_0", "acc0_256")[b]) for b in range(2)]
+        power_sb = keep.tile([P, 2, P], F32, name="power_sb", align_bytes=64)
+        csq_t = keep.tile([P, 2, P], F32, name="csq_t", align_bytes=64)
+        rs = keep.tile([P, V], F32, name="rs")
+        inv = keep.tile([P, V], F32, name="inv")
+        c_t = [psum.tile([P, P], F32, name=f"c_t{b}", tag=("acc0_0", "acc0_256")[b]) for b in range(2)]
+        det = [psum.tile([P, P], F32, name=f"det{b}", tag=("acc0_384", "acc1_0")[b]) for b in range(2)]
         prod = keep.tile([P, V], F32, name="prod")
         num = keep.tile([P, V], F32, name="num")
         res = keep.tile([P, V], F32, name="res")
-        for t in range(2):
-            for b in range(2):
-                nc.vector.tensor_tensor(pc[b][:, t, :], g[:, t, blocks[b]], g[:, 2 + t, blocks[b]], ALU.mult)
         for b in range(2):
-            nc.vector.tensor_tensor(c[:, blocks[b]], pc[b][:, 0, :], pc[b][:, 1, :], ALU.subtract)
-            nc.scalar.activation(csq[:, blocks[b]], c[:, blocks[b]], ACT.Square)
-            nc.tensor.matmul(det_t[b][:], csq[:, blocks[b]], ident[:], is_transpose=True, start=False, stop=True)
+            nc.vector.tensor_tensor(pc[:, 0, blocks[b]], g[:, 0, blocks[b]], g[:, 2, blocks[b]], ALU.mult)
+            nc.tensor.matmul(c_t[b][:], pc[:, 0, blocks[b]], ident[:], is_transpose=True, start=True, stop=False)
         for b in range(2):
-            nc.scalar.activation(rs_t[:, b, :], det_t[b][:], ACT.Abs_reciprocal_sqrt)
+            nc.vector.scalar_tensor_tensor(pc[:, 1, blocks[b]], g[:, 1, blocks[b]], (minus[:, 0:1], -1.0)[b], g[:, 3, blocks[b]], ALU.mult, ALU.mult)
+            nc.tensor.matmul(c_t[b][:], pc[:, 1, blocks[b]], ident[:], is_transpose=True, start=False, stop=True)
         for b in range(2):
-            nc.scalar.activation(inv_t[:, b, :], rs_t[:, b, :], ACT.Square)
-            nc.tensor.transpose(inv[b][:], inv_t[:, b, :], ident[:])
-        late = keep.tile([P, 4, V], F32, name="late", tag="held")
-        pd = late[:, 0:2, :]
-        pm = late[:, 2:4, :]
-        nc.vector.tensor_tensor(pd, rx[:], g[:, 2:4, :], ALU.mult)
-        nc.vector.tensor_tensor(pm, rx[:], g[:, 0:2, :], ALU.mult)
-        nc.vector.tensor_tensor(d[:], pd[:, 0, :], pd[:, 1, :], ALU.subtract)
-        nc.vector.tensor_tensor(ma[:], pm[:, 0, :], pm[:, 1, :], ALU.add)
+            nc.scalar.copy(power_sb[:, b, :], power_t[b][:])
+            nc.tensor.matmul(det[b][:], power_sb[:, b, :], ident[:], is_transpose=True, start=True, stop=False)
+        for b in range(2):
+            nc.scalar.activation(csq_t[:, b, :], c_t[b][:], ACT.Square)
+            nc.tensor.matmul(det[b][:], csq_t[:, b, :], ident[:], is_transpose=True, start=False, stop=True)
+        for b in range(2):
+            nc.scalar.activation(rs[:, blocks[b]], det[b][:], ACT.Abs_reciprocal_sqrt, bias=noise2[:, 0:1])
+        for b in range(2):
+            nc.scalar.activation(inv[:, blocks[b]], rs[:, blocks[b]], ACT.Square)
+        late = keep.tile([P, 2, V], F32, name="late", tag="held")
+        nc.vector.tensor_tensor(late[:, 0, :], rx[:, 0, :], g[:, 2, :], ALU.mult)
+        nc.vector.tensor_tensor(late[:, 1, :], rx[:, 1, :], g[:, 1, :], ALU.mult)
+        nc.vector.tensor_tensor(c[:], pc[:, 0, :], pc[:, 1, :], ALU.add)
+        nc.vector.tensor_tensor(d[:], late[:, 0, :], early[:, 1, :], ALU.subtract)
+        nc.vector.tensor_tensor(ma[:], early[:, 0, :], late[:, 1, :], ALU.add)
         for b in range(2):
             nc.vector.tensor_tensor(prod[:, blocks[b]], c[:, blocks[b]], d[:, blocks[b]], ALU.mult)
         for b in range(2):
             nc.vector.scalar_tensor_tensor(num[:, blocks[b]], ma[:, blocks[b]], noise_sb[:, 0:1], prod[:, blocks[b]], ALU.mult, ALU.add)
         for b, queue in enumerate((nc.sync, nc.scalar)):
-            nc.vector.tensor_tensor(res[:, blocks[b]], num[:, blocks[b]], inv[b][:], ALU.mult)
+            nc.vector.tensor_tensor(res[:, blocks[b]], num[:, blocks[b]], inv[:, blocks[b]], ALU.mult)
             queue.dma_start(out[:, blocks[b]], res[:, blocks[b]])

from contextlib import ExitStack

import concourse.mybir as mybir
from concourse.masks import make_identity

K, T, S, N, V = 512, 1024, 512, 128, 256
FLOPS = 2 * 2 * K * N * S

F32 = mybir.dt.float32
BF16 = mybir.dt.bfloat16
I32 = mybir.dt.int32
U32 = mybir.dt.uint32
U16 = mybir.dt.uint16
U8 = mybir.dt.uint8
FP8X4 = mybir.dt.float8_e4m3fn_x4
ALU = mybir.AluOpType
ACT = mybir.ActivationFunctionType

P = 128


def tile_picked_ylmm2_est_p_kernel(tc, x_words, x_scales, w1, w2, noise, rxa, rxb, offs, st1, st2, out):
    nc = tc.nc
    with ExitStack() as ctx:
        keep = ctx.enter_context(tc.tile_pool(name="keep", bufs=1))
        psum = ctx.enter_context(tc.psum_pool(name="psum", bufs=1))

        offs_sb = keep.tile([P, S // 16], U16, name="offs_sb")
        st1_sb = keep.tile([P, V // 16], U16, name="st1_sb")
        st2_sb = keep.tile([P, V // 16], U16, name="st2_sb")
        words_all = keep.tile([P, T], U32, name="words_all", align_bytes=64)
        scales_all = keep.tile([P, T], U8, name="scales_all", align_bytes=64)
        w_raw = [keep.tile([P, 4, N], F32, name=f"w_raw{i}", align_bytes=64) for i in range(2)]
        noise_sb = keep.tile([P, 1], F32, name="noise_sb")
        rx = keep.tile([P, 2, V], F32, name="rx")

        ident = keep.tile([P, P], F32, name="ident", align_bytes=64)
        nc.vector.memset(scales_all[:].bitcast(I32), 0)
        nc.sync.dma_start(offs_sb[:], offs)
        nc.sync.dma_start(noise_sb[:], noise)
        for q, queue in enumerate((nc.sync, nc.sync, nc.scalar, nc.scalar)):
            queue.dma_start(scales_all[32 * q : 32 * q + 4, :].bitcast(I32), x_scales[0, 4 * q : 4 * q + 4, :].bitcast(I32))
        nc.sync.dma_start(w_raw[0][:], w1.rearrange("(p j) n -> p j n", j=4))
        nc.sync.dma_start(words_all[:].bitcast(I32), x_words[0].rearrange("p c r -> p (c r)").bitcast(I32))
        nc.sync.dma_start(w_raw[1][:], w2.rearrange("(p j) n -> p j n", j=4))
        nc.sync.dma_start(st1_sb[:], st1)
        nc.sync.dma_start(st2_sb[:], st2)
        nc.sync.dma_start(rx[:, 0, :], rxa)
        nc.sync.dma_start(rx[:, 1, :], rxb)
        nc.vector.memset(ident[:], 0.0)
        make_identity(nc, ident[:], nomemset=True)
        minus = keep.tile([P, 1], F32, name="minus", tag="held")
        nc.vector.memset(minus[:], -1.0)

        inv_root = keep.tile([P, 1], F32, name="inv_root")
        root = keep.tile([P, 1], F32, name="root")
        noise2 = keep.tile([P, 1], F32, name="noise2")
        nc.scalar.activation(inv_root[:], noise_sb[:], ACT.Abs_reciprocal_sqrt, bias=1e-30)
        nc.scalar.activation(noise2[:], noise_sb[:], ACT.Square)
        nc.scalar.activation(root[:], inv_root[:], ACT.Copy, scale=noise_sb[:, 0:1])

        x_sc = keep.tile([P, S], U8, name="x_sc", align_bytes=64)
        nc.vector.tensor_copy(x_sc[:], scales_all[:].indirect(offs_sb[:]))

        w_bf = [keep.tile([P, N, 4], BF16, name=f"w_bf{i}", align_bytes=64) for i in range(2)]
        w_q = [keep.tile([P, N], U32, name=f"w_q{i}", align_bytes=64) for i in range(2)]
        w_sc = [keep.tile([P, N], U8, name=f"w_sc{i}", align_bytes=64) for i in range(2)]
        x_q = keep.tile([P, S], U32, name="x_q", align_bytes=64)
        h_sb = [keep.tile([P, S], F32, name=f"h_sb{i}", align_bytes=64) for i in range(2)]
        for i in range(2):
            nc.scalar.copy(w_bf[i][:], w_raw[i][:].rearrange("p j n -> p n j"))

        def quantize(i):
            nc.vector.quantize_mx(out=w_q[i][:].bitcast(FP8X4), scales=w_sc[i][:], in_=w_bf[i][:].rearrange("p n j -> p (n j)"))

        def pick(cols):
            nc.vector.tensor_copy(x_q[:, cols], words_all[:].indirect(offs_sb[:, cols.start // 16 : cols.stop // 16]))

        def product(i, cols):
            acc = psum.tile([P, cols.stop - cols.start], F32, name=f"acc{i}_{cols.start}")
            nc.tensor.matmul_mx(out=acc[:], lhsT=w_q[i][:].bitcast(FP8X4), lhsT_scale=w_sc[i][:], rhs=x_q[:, cols].bitcast(FP8X4), rhs_scale=x_sc[:, cols], start=True, stop=True)
            nc.scalar.copy(h_sb[i][:, cols], acc[:])

        pieces = (slice(0, 256), slice(256, 384), slice(384, 512))
        quantize(0)
        for cols in pieces:
            pick(cols)
            product(0, cols)
        quantize(1)
        product(1, slice(0, 256))
        product(1, slice(256, 512))


        g = keep.tile([P, 4, V], F32, name="g")
        sq = keep.tile([P, 4, V], F32, name="sq", align_bytes=64)
        power_t = [psum.tile([P, P], F32, name=f"power_t{b}") for b in range(2)]
        blocks = [slice(b * P, (b + 1) * P) for b in range(2)]
        order = ((0, 0, st1_sb), (3, 0, st2_sb), (2, 1, st2_sb), (1, 1, st1_sb))
        for n, (slot, i, lst) in enumerate(order):
            nc.vector.tensor_copy(g[:, slot, :], h_sb[i][:].indirect(lst[:]))
            nc.scalar.activation(sq[:, slot, :], g[:, slot, :], ACT.Square, scale=root[:, 0:1])
            for b in range(2):
                nc.tensor.matmul(power_t[b][:], sq[:, slot, blocks[b]], ident[:], is_transpose=True, start=(n == 0), stop=(n == 3))

        early = keep.tile([P, 2, V], F32, name="early")
        nc.gpsimd.tensor_tensor(early[:, 0, :], rx[:, 0, :], g[:, 0, :], ALU.mult)
        nc.gpsimd.tensor_tensor(early[:, 1, :], rx[:, 1, :], g[:, 3, :], ALU.mult)
        pc = keep.tile([P, 2, V], F32, name="pc", align_bytes=64)
        c = keep.tile([P, V], F32, name="c")
        d = keep.tile([P, V], F32, name="d")
        ma = keep.tile([P, V], F32, name="ma")
        power_sb = keep.tile([P, 2, P], F32, name="power_sb", align_bytes=64)
        csq_t = keep.tile([P, 2, P], F32, name="csq_t", align_bytes=64)
        rs = keep.tile([P, V], F32, name="rs")
        inv = keep.tile([P, V], F32, name="inv")
        c_t = [psum.tile([P, P], F32, name=f"c_t{b}", tag=("acc0_0", "acc0_256")[b]) for b in range(2)]
        det = [psum.tile([P, P], F32, name=f"det{b}", tag=("acc0_384", "acc1_0")[b]) for b in range(2)]
        prod = keep.tile([P, V], F32, name="prod")
        num = keep.tile([P, V], F32, name="num")
        res = keep.tile([P, V], F32, name="res")
        for b in range(2):
            nc.vector.tensor_tensor(pc[:, 0, blocks[b]], g[:, 0, blocks[b]], g[:, 2, blocks[b]], ALU.mult)
            nc.tensor.matmul(c_t[b][:], pc[:, 0, blocks[b]], ident[:], is_transpose=True, start=True, stop=False)
        for b in range(2):
            nc.vector.scalar_tensor_tensor(pc[:, 1, blocks[b]], g[:, 1, blocks[b]], (minus[:, 0:1], -1.0)[b], g[:, 3, blocks[b]], ALU.mult, ALU.mult)
            nc.tensor.matmul(c_t[b][:], pc[:, 1, blocks[b]], ident[:], is_transpose=True, start=False, stop=True)
        for b in range(2):
            nc.scalar.copy(power_sb[:, b, :], power_t[b][:])
            nc.tensor.matmul(det[b][:], power_sb[:, b, :], ident[:], is_transpose=True, start=True, stop=False)
        for b in range(2):
            nc.scalar.activation(csq_t[:, b, :], c_t[b][:], ACT.Square)
            nc.tensor.matmul(det[b][:], csq_t[:, b, :], ident[:], is_transpose=True, start=False, stop=True)
        for b in range(2):
            nc.scalar.activation(rs[:, blocks[b]], det[b][:], ACT.Abs_reciprocal_sqrt, bias=noise2[:, 0:1])
        for b in range(2):
            nc.scalar.activation(inv[:, blocks[b]], rs[:, blocks[b]], ACT.Square)
        late = keep.tile([P, 2, V], F32, name="late", tag="held")
        nc.vector.tensor_tensor(late[:, 0, :], rx[:, 0, :], g[:, 2, :], ALU.mult)
        nc.vector.tensor_tensor(late[:, 1, :], rx[:, 1, :], g[:, 1, :], ALU.mult)
        nc.vector.tensor_tensor(c[:], pc[:, 0, :], pc[:, 1, :], ALU.add)
        nc.vector.tensor_tensor(d[:], late[:, 0, :], early[:, 1, :], ALU.subtract)
        nc.vector.tensor_tensor(ma[:], early[:, 0, :], late[:, 1, :], ALU.add)
        for b in range(2):
            nc.vector.tensor_tensor(prod[:, blocks[b]], c[:, blocks[b]], d[:, blocks[b]], ALU.mult)
        for b in range(2):
            nc.vector.scalar_tensor_tensor(num[:, blocks[b]], ma[:, blocks[b]], noise_sb[:, 0:1], prod[:, blocks[b]], ALU.mult, ALU.add)
        for b, queue in enumerate((nc.sync, nc.scalar)):
            nc.vector.tensor_tensor(res[:, blocks[b]], num[:, blocks[b]], inv[:, blocks[b]], ALU.mult)
            queue.dma_start(out[:, blocks[b]], res[:, blocks[b]])
